import numpy as np
import ml_dtypes


def mxq(x, axis, fmt="e4m3"):
    dtype, down = {"e4m3": (ml_dtypes.float8_e4m3fn, 7), "e5m2": (ml_dtypes.float8_e5m2, 14)}[fmt]
    v = np.moveaxis(np.asarray(x, np.float32).astype(ml_dtypes.bfloat16).astype(np.float64), axis, -1)
    blocks = v.reshape(v.shape[:-1] + (-1, 32))
    amax = np.abs(blocks).max(-1, keepdims=True)
    byte = np.maximum(np.where(amax > 0, np.frexp(amax)[1] - 1 + 127, 0) - down, 1)
    scale = np.exp2(byte - 127.0)
    codes = (blocks / scale).astype(np.float32).astype(dtype).astype(np.float64)
    return np.moveaxis((codes * scale).reshape(v.shape), -1, axis)


WIDE = False


def mx_kscale(k):
    if not WIDE:
        return np.ones(k)
    levels = np.array([10, -10, 5, -5, 0])
    if k % 512:
        return np.exp2(np.random.permutation(np.resize(levels, k // 32))).repeat(32)
    a = np.empty((k // 512, 16))
    for p in range(k // 512):
        a[p, :8] = np.random.permutation(np.resize(levels, 8))
        for g in range(8):
            far = levels[np.abs(levels - a[p, g]) >= 10]
            a[p, g + 8] = far[np.random.randint(len(far))]
    return np.exp2(a.ravel()).repeat(32)


def f64(x):
    return np.asarray(x).astype(np.float64)


def striped(idx):
    return np.tile(idx.reshape(-1, 16).T, (8, 1)).astype(np.uint16)


def unstriped(offs):
    return offs[:16].T.reshape(-1).astype(np.int64)


E2M1 = np.array([0.0, 0.5, 1.0, 1.5, 2.0, 3.0, 4.0, 6.0, -0.0, -0.5, -1.0, -1.5, -2.0, -3.0, -4.0, -6.0])


def pack_weight(w, fmt):
    k, n = w.shape
    w = f64(np.asarray(w, np.float32).astype(ml_dtypes.bfloat16)).reshape(k // 32, 32, n)
    amax = np.abs(w).max(1)
    if fmt == "e4m3":
        byte = np.frexp(amax)[1] - 1 + 127 - 7
    else:
        mant, ex = np.frexp(amax / 6.0)
        byte = np.where(mant > 0.5, ex, ex - 1) + 127
    byte = np.clip(np.where(amax > 0, byte, 1), 1, 254)
    scaled = (w * np.exp2(127.0 - byte)[:, None, :]).reshape(k, n).astype(np.float32)
    by_word = np.ascontiguousarray(scaled.reshape(k // 512, 128, 4, n).transpose(0, 1, 3, 2))
    if fmt == "e4m3":
        words = by_word.astype(ml_dtypes.float8_e4m3fn).view(np.uint8)
    else:
        c = by_word.astype(ml_dtypes.float4_e2m1fn).view(np.uint8) & 0xF
        words = (c[..., 0::2] | (c[..., 1::2] << 4)).reshape(k // 512, 128, 2 * n)
    return np.ascontiguousarray(words), np.ascontiguousarray(byte.astype(np.uint8).reshape(k // 512, 16, n))


def unpack_weight(words, scales, fmt):
    g, _, n = scales.shape
    words = np.ascontiguousarray(words).reshape(g, 128, n, -1)
    if fmt == "e4m3":
        vals = words.view(ml_dtypes.float8_e4m3fn).astype(np.float64)
    else:
        nib = np.empty((g, 128, n, 4), np.uint8)
        nib[..., 0::2] = words & 0xF
        nib[..., 1::2] = words >> 4
        vals = E2M1[nib]
    vals = vals * np.repeat(np.exp2(scales.astype(np.float64) - 127.0), 8, axis=1)[..., None]
    return vals.transpose(0, 1, 3, 2).reshape(g * 512, n)


def gelu(v):
    return 0.5 * v * (1.0 + np.tanh(np.sqrt(2.0 / np.pi) * (v + 0.044715 * v**3)))


K, T, E, N = 1536, 1024, 4, 256
COUNTS = (384, 128, 256, 256)
STARTS = np.cumsum((0,) + COUNTS)
K8 = 512


def by_expert(wq, xq):
    return np.concatenate([wq[e].T @ xq[:, STARTS[e]:STARTS[e + 1]] for e in range(E)], axis=1)


def setup_inputs():
    n = np.random.standard_normal
    s = mx_kscale(K)[:, None]
    expert = np.random.permutation(np.repeat(np.arange(E), COUNTS))
    slot_token = np.argsort(expert, kind="stable")
    w = n((E, K, N)) / np.sqrt(K) / s[None]
    w8 = [pack_weight(m[:K8], "e4m3") for m in w]
    w4 = [pack_weight(m[K8:], "e2m1") for m in w]
    return {
        "xT": (n((K, T)) * s).astype(np.float32),
        "w8_words": np.stack([m[0] for m in w8]),
        "w8_scales": np.stack([m[1] for m in w8]),
        "w4_words": np.stack([m[0] for m in w4]),
        "w4_scales": np.stack([m[1] for m in w4]),
        "b": (0.3 * n((N, E))).astype(np.float32),
        "gate": np.tile(np.random.uniform(0.2, 1.0, T), (N, 1)).astype(np.float32),
        "offs": striped(slot_token),
    }


def reference(xT, w8_words, w8_scales, w4_words, w4_scales, b, gate, offs):
    idx = unstriped(offs)
    w = np.stack([np.concatenate([unpack_weight(w8_words[e], w8_scales[e], "e4m3"), unpack_weight(w4_words[e], w4_scales[e], "e2m1")]) for e in range(E)])
    xq = mxq(f64(xT)[:, idx], 0, "e4m3")
    y = by_expert(w, xq)
    y = gelu(y + np.repeat(f64(b), COUNTS, axis=1))
    out = np.zeros((N, T))
    out[:, idx] = f64(gate) * y
    return out

@@ -1,0 +1,181 @@
+from contextlib import ExitStack
+
+import concourse.mybir as mybir
+
+F32 = mybir.dt.float32
+BF16 = mybir.dt.bfloat16
+I32 = mybir.dt.int32
+U32 = mybir.dt.uint32
+U16 = mybir.dt.uint16
+U8 = mybir.dt.uint8
+FP8X4 = mybir.dt.float8_e4m3fn_x4
+FP4X4 = mybir.dt.float4_e2m1fn_x4
+ACT = mybir.ActivationFunctionType
+MULT = mybir.AluOpType.mult
+
+K, T, E, N = 1536, 1024, 4, 256
+COUNTS = (384, 128, 256, 256)
+STARTS = (0, 384, 512, 768)
+P = 128
+HALF = 512
+CHUNK = 128
+
+FLOPS = 2 * K * N * T
+BYTES = 4 * K * T + E * (512 * N + 1024 * N // 2 + 48 * N) + 4 * N * E + 4 * T + 2 * P * 64 + 4 * N * T
+
+
+def expert_of(slot):
+    return max(e for e in range(E) if STARTS[e] <= slot)
+
+
+def tile_moe_rag_lin_gelu_kernel(
+    tc, xT, w8_words, w8_scales, w4_words, w4_scales, b, gate, offs, out
+):
+    nc = tc.nc
+    with ExitStack() as ctx:
+        keep = ctx.enter_context(tc.tile_pool(name="keep", bufs=1))
+        psum = ctx.enter_context(tc.psum_pool(name="psum", bufs=8))
+
+        offsets = keep.tile([P, T // 16], U16, name="offsets")
+
+        warm = keep.tile([P, 1], F32, name="warm")
+        warm_out = keep.tile([P, 1], F32, name="warm_out")
+        bytes01 = keep.tile([P, T], U8, name="bytes01", align_bytes=64)
+        bytes2 = keep.tile([P, T], U8, name="bytes2", align_bytes=64)
+        s8 = keep.tile([P, E, N], U8, name="s8", align_bytes=64)
+        s4 = keep.tile([P, 2 * E, N], U8, name="s4", align_bytes=64)
+        nc.gpsimd.memset(warm[:], 0.0)
+        nc.gpsimd.memset(bytes01[:].bitcast(I32), 0)
+        nc.gpsimd.memset(s8[:].rearrange("p e n -> p (e n)").bitcast(I32), 0)
+        nc.gpsimd.memset(s4[:].rearrange("p e n -> p (e n)").bitcast(I32), 0)
+        nc.gpsimd.memset(bytes2[:].bitcast(I32), 0)
+        nc.scalar.activation(warm_out[:], warm[:], ACT.Gelu_apprx_tanh)
+
+        x_cols = ((0, HALF), (HALF, T)), ((0, HALF), (HALF, T)), ((0, HALF), (HALF, T))
+        x_raw = []
+        for a in range(3):
+            rows = xT[512 * a : 512 * (a + 1), :].rearrange("(p j) t -> p j t", j=4)
+            parts = []
+            for lo, hi in x_cols[a]:
+                raw = keep.tile([P, 4, hi - lo], F32, name=f"raw{a}_{lo}")
+                nc.sync.dma_start(raw[:], rows[:, :, lo:hi])
+                parts.append((lo, hi, raw))
+            x_raw.append(parts)
+            if a == 0:
+                nc.sync.dma_start(offsets[:], offs)
+            if a == 1:
+                w4s = w4_scales.rearrange("e a q n -> (e a) q n")
+                for q in range(4):
+                    src = w8_scales[:, 0, 4 * q : 4 * q + 4, :].bitcast(I32)
+                    nc.sync.dma_start(s8[32 * q : 32 * q + 4, :, :].bitcast(I32), src.rearrange("e r n -> r e n"))
+                for q in range(4):
+                    src = w4s[:, 4 * q : 4 * q + 4, :].bitcast(I32)
+                    nc.sync.dma_start(s4[32 * q : 32 * q + 4, :, :].bitcast(I32), src.rearrange("g r n -> r g n"))
+        bias = keep.tile([P, 2, E], F32, name="bias")
+        nc.scalar.dma_start(bias[:], b.rearrange("(m p) e -> p m e", p=P))
+        w8 = keep.tile([P, E, 4 * N], U8, name="w8", align_bytes=64)
+        w4 = keep.tile([P, E, 2, 2 * N], U8, name="w4", align_bytes=64)
+        gates = keep.tile([P, T], F32, name="gates")
+        for e in range(E):
+            nc.sync.dma_start(w8[:, e, :].bitcast(I32), w8_words[e, 0].rearrange("p n r -> p (n r)").bitcast(I32))
+            nc.sync.dma_start(w4[:, e, :, :].bitcast(I32), w4_words[e].bitcast(I32).rearrange("a p x -> p a x"))
+            if e == 1:
+                nc.sync.dma_start(gates[:, 0:HALF], gate[0:P, 0:HALF])
+        nc.sync.dma_start(gates[:, HALF:T], gate[0:P, HALF:T])
+
+        picked01 = keep.tile([P, T], U8, name="picked01", align_bytes=64)
+        picked2 = keep.tile([P, T], U8, name="picked2", align_bytes=64)
+        words = []
+        picked_words = []
+        for a in range(3):
+            w_all = keep.tile([P, T], U32, name=f"words{a}", align_bytes=64)
+            picked = keep.tile([P, T], U32, name=f"picked_words{a}", align_bytes=64)
+            words.append(w_all)
+            picked_words.append(picked)
+        scalar_share = {(2, 1): 192}
+
+        def group_and_quantize(a, h):
+            plane = (bytes01[4:P, :], bytes01[:], bytes2[:])[a]
+            lo = HALF * h
+            grouped = keep.tile([P, HALF, 4], BF16, name=f"grouped{a}_{h}", align_bytes=64)
+            part = [r for r in x_raw[a] if r[0] <= lo < r[1]][0]
+            raw, base = part[2], lo - part[0]
+            cut = scalar_share.get((a, h), 512)
+            for engine, u, v in ((nc.scalar, 0, cut), (nc.vector, cut, HALF)):
+                if u == v:
+                    continue
+                dst = grouped[:, u:v, :].rearrange("p (c i) j -> p c j i", i=4)
+                srcv = raw[:, :, base + u : base + v].rearrange("p j (c i) -> p c j i", i=4)
+                if engine is nc.scalar:
+                    nc.scalar.copy(dst, srcv)
+                else:
+                    nc.vector.tensor_copy(dst, srcv)
+            nc.vector.quantize_mx(
+                out=words[a][:, lo : lo + HALF].bitcast(FP8X4),
+                scales=plane[:, lo : lo + HALF],
+                in_=grouped[:].rearrange("p t j -> p (t j)"),
+            )
+
+        def pick(dst, src, h):
+            nc.vector.tensor_copy(dst[:, HALF * h : HALF * (h + 1)], src[:].indirect(offsets[:, 32 * h : 32 * (h + 1)]))
+
+        group_and_quantize(0, 0)
+        group_and_quantize(0, 1)
+        group_and_quantize(1, 0)
+        pick(picked_words[0], words[0], 0)
+        pick(picked_words[0], words[0], 1)
+        group_and_quantize(1, 1)
+        group_and_quantize(2, 0)
+        pick(picked_words[1], words[1], 0)
+        pick(picked_words[1], words[1], 1)
+        pick(picked01, bytes01, 0)
+        pick(picked01, bytes01, 1)
+        group_and_quantize(2, 1)
+        for h in range(2):
+            pick(picked_words[2], words[2], h)
+            pick(picked2, bytes2, h)
+
+        def multiply(acc, m, slot, a):
+            e = expert_of(slot)
+            n_cols = slice(P * m, P * (m + 1))
+            s_cols = slice(slot, slot + CHUNK)
+            if a == 0:
+                lhs = w8[:, e, 4 * P * m : 4 * P * (m + 1)].bitcast(FP8X4)
+                lhs_scale = s8[:, e, n_cols]
+            else:
+                lhs = w4[:, e, a - 1, 2 * P * m : 2 * P * (m + 1)].bitcast(FP4X4)
+                lhs_scale = s4[:, 2 * e + a - 1, n_cols]
+            nc.tensor.matmul_mx(
+                out=acc,
+                lhsT=lhs,
+                lhsT_scale=lhs_scale,
+                rhs=picked_words[a][:, s_cols].bitcast(FP8X4),
+                rhs_scale=(picked01[4:P, s_cols], picked01[:, s_cols], picked2[:, s_cols])[a],
+                start=(a == 0),
+                stop=(a == 2),
+            )
+
+        y = [keep.tile([P, T], F32, name=f"y{m}") for m in range(2)]
+        gated = [keep.tile([P, T], F32, name=f"gated{m}") for m in range(2)]
+        result = [keep.tile([P, T], F32, name=f"result{m}") for m in range(2)]
+        for h in range(2):
+            accs = {}
+            for m in range(2):
+                for slot in range(HALF * h, HALF * (h + 1), CHUNK):
+                    acc = psum.tile([P, CHUNK], F32, name="acc")
+                    multiply(acc[:], m, slot, 0)
+                    multiply(acc[:], m, slot, 1)
+                    accs[m, slot] = acc
+            for m in range(2):
+                for slot in range(HALF * h, HALF * (h + 1), CHUNK):
+                    multiply(accs[m, slot][:], m, slot, 2)
+                    e = expert_of(slot)
+                    nc.scalar.activation(y[m][:, slot : slot + CHUNK], accs[m, slot][:], ACT.Gelu_apprx_tanh, bias=bias[:, m, e : e + 1])
+                    if slot % 256 == 128:
+                        cols = slice(slot - 128, slot + 128)
+                        nc.gpsimd.tensor_tensor(gated[m][:, cols], y[m][:, cols], gates[:, cols], MULT)
+            for m in range(2):
+                cols = slice(HALF * h, HALF * (h + 1))
+                nc.vector.tensor_copy(result[m][:].indirect(offsets[:, 32 * h : 32 * (h + 1)]), gated[m][:, cols])
+        for m in range(2):
+            nc.sync.dma_start(out[P * m : P * (m + 1), :], result[m][:])

@@ -156,7 +156,6 @@ def tile_moe_rag_lin_gelu_kernel(
             )
 
         y = [keep.tile([P, T], F32, name=f"y{m}") for m in range(2)]
-        gated = [keep.tile([P, T], F32, name=f"gated{m}") for m in range(2)]
         result = [keep.tile([P, T], F32, name=f"result{m}") for m in range(2)]
         for h in range(2):
             accs = {}
@@ -171,11 +170,8 @@ def tile_moe_rag_lin_gelu_kernel(
                     multiply(accs[m, slot][:], m, slot, 2)
                     e = expert_of(slot)
                     nc.scalar.activation(y[m][:, slot : slot + CHUNK], accs[m, slot][:], ACT.Gelu_apprx_tanh, bias=bias[:, m, e : e + 1])
-                    if slot % 256 == 128:
-                        cols = slice(slot - 128, slot + 128)
-                        nc.gpsimd.tensor_tensor(gated[m][:, cols], y[m][:, cols], gates[:, cols], MULT)
             for m in range(2):
                 cols = slice(HALF * h, HALF * (h + 1))
-                nc.vector.tensor_copy(result[m][:].indirect(offsets[:, 32 * h : 32 * (h + 1)]), gated[m][:, cols])
+                nc.vector.tensor_tensor(result[m][:].indirect(offsets[:, 32 * h : 32 * (h + 1)]), y[m][:, cols], gates[:, cols], MULT)
         for m in range(2):
             nc.sync.dma_start(out[P * m : P * (m + 1), :], result[m][:])

@@ -19,6 +19,8 @@ STARTS = (0, 384, 512, 768)
 P = 128
 HALF = 512
 CHUNK = 128
+ORDER = (1, 2, 0)
+CHUNKS = (((0, 512, 192), (512, 512, 192),), ((0, 512, 448), (512, 512, 384),), ((0, 512, 448), (512, 256, 192), (768, 256, 160),))
 
 FLOPS = 2 * K * N * T
 BYTES = 4 * K * T + E * (512 * N + 1024 * N // 2 + 48 * N) + 4 * N * E + 4 * T + 2 * P * 64 + 4 * N * T
@@ -40,138 +42,134 @@ def tile_moe_rag_lin_gelu_kernel(
 
         warm = keep.tile([P, 1], F32, name="warm")
         warm_out = keep.tile([P, 1], F32, name="warm_out")
-        bytes01 = keep.tile([P, T], U8, name="bytes01", align_bytes=64)
-        bytes2 = keep.tile([P, T], U8, name="bytes2", align_bytes=64)
+        bytes_a = keep.tile([P, T], U8, name="bytes_a", align_bytes=64)
+        bytes_bc = keep.tile([P, T], U8, name="bytes_bc", align_bytes=64)
         s8 = keep.tile([P, E, N], U8, name="s8", align_bytes=64)
         s4 = keep.tile([P, 2 * E, N], U8, name="s4", align_bytes=64)
         nc.gpsimd.memset(warm[:], 0.0)
-        nc.gpsimd.memset(bytes01[:].bitcast(I32), 0)
-        nc.gpsimd.memset(s8[:].rearrange("p e n -> p (e n)").bitcast(I32), 0)
+        nc.gpsimd.memset(bytes_a[:].bitcast(I32), 0)
+        nc.gpsimd.memset(bytes_bc[:].bitcast(I32), 0)
         nc.gpsimd.memset(s4[:].rearrange("p e n -> p (e n)").bitcast(I32), 0)
-        nc.gpsimd.memset(bytes2[:].bitcast(I32), 0)
+        nc.gpsimd.memset(s8[:].rearrange("p e n -> p (e n)").bitcast(I32), 0)
         nc.scalar.activation(warm_out[:], warm[:], ACT.Gelu_apprx_tanh)
 
-        x_cols = ((0, HALF), (HALF, T)), ((0, HALF), (HALF, T)), ((0, HALF), (HALF, T))
-        x_raw = []
-        for a in range(3):
+        raws = {}
+        for i, a in enumerate(ORDER):
             rows = xT[512 * a : 512 * (a + 1), :].rearrange("(p j) t -> p j t", j=4)
-            parts = []
-            for lo, hi in x_cols[a]:
-                raw = keep.tile([P, 4, hi - lo], F32, name=f"raw{a}_{lo}")
-                nc.sync.dma_start(raw[:], rows[:, :, lo:hi])
-                parts.append((lo, hi, raw))
-            x_raw.append(parts)
-            if a == 0:
+            for lo, width, scalar in CHUNKS[i]:
+                raw = keep.tile([P, 4, width], F32, name=f"raw{i}_{lo}")
+                nc.sync.dma_start(raw[:], rows[:, :, lo : lo + width])
+                raws[i, lo] = raw
+            if i == 0:
                 nc.sync.dma_start(offsets[:], offs)
-            if a == 1:
-                w4s = w4_scales.rearrange("e a q n -> (e a) q n")
-                for q in range(4):
-                    src = w8_scales[:, 0, 4 * q : 4 * q + 4, :].bitcast(I32)
-                    nc.sync.dma_start(s8[32 * q : 32 * q + 4, :, :].bitcast(I32), src.rearrange("e r n -> r e n"))
-                for q in range(4):
-                    src = w4s[:, 4 * q : 4 * q + 4, :].bitcast(I32)
-                    nc.sync.dma_start(s4[32 * q : 32 * q + 4, :, :].bitcast(I32), src.rearrange("g r n -> r g n"))
-        bias = keep.tile([P, 2, E], F32, name="bias")
-        nc.scalar.dma_start(bias[:], b.rearrange("(m p) e -> p m e", p=P))
+        w4s = w4_scales.rearrange("e a q n -> (e a) q n")
+        for q in range(4):
+            src = w4s[:, 4 * q : 4 * q + 4, :].bitcast(I32)
+            nc.sync.dma_start(s4[32 * q : 32 * q + 4, :, :].bitcast(I32), src.rearrange("g r n -> r g n"))
+        for q in range(4):
+            src = w8_scales[:, 0, 4 * q : 4 * q + 4, :].bitcast(I32)
+            nc.sync.dma_start(s8[32 * q : 32 * q + 4, :, :].bitcast(I32), src.rearrange("e r n -> r e n"))
         w8 = keep.tile([P, E, 4 * N], U8, name="w8", align_bytes=64)
         w4 = keep.tile([P, E, 2, 2 * N], U8, name="w4", align_bytes=64)
         gates = keep.tile([P, T], F32, name="gates")
-        for e in range(E):
-            nc.sync.dma_start(w8[:, e, :].bitcast(I32), w8_words[e, 0].rearrange("p n r -> p (n r)").bitcast(I32))
-            nc.sync.dma_start(w4[:, e, :, :].bitcast(I32), w4_words[e].bitcast(I32).rearrange("a p x -> p a x"))
-            if e == 1:
-                nc.sync.dma_start(gates[:, 0:HALF], gate[0:P, 0:HALF])
-        nc.sync.dma_start(gates[:, HALF:T], gate[0:P, HALF:T])
+        bias = keep.tile([P, 2, E], F32, name="bias")
+        for h in range(2):
+            es = slice(2 * h, 2 * h + 2)
+            nc.sync.dma_start(
+                w4[:, es, :, :].rearrange("p e a x -> p (e a) x").bitcast(I32),
+                w4_words.rearrange("e a p x -> (e a) p x")[4 * h : 4 * h + 4].bitcast(I32).rearrange("g p x -> p g x"),
+            )
+            nc.sync.dma_start(
+                w8[:, es, :].bitcast(I32),
+                w8_words[es, 0].rearrange("e p n r -> e p (n r)").bitcast(I32).rearrange("e p x -> p e x"),
+            )
+            if h == 0:
+                nc.sync.dma_start(bias[:], b.rearrange("(m p) e -> p m e", p=P))
+            nc.sync.dma_start(gates[:, HALF * h : HALF * (h + 1)], gate[0:P, HALF * h : HALF * (h + 1)])
 
-        picked01 = keep.tile([P, T], U8, name="picked01", align_bytes=64)
-        picked2 = keep.tile([P, T], U8, name="picked2", align_bytes=64)
-        words = []
-        picked_words = []
-        for a in range(3):
-            w_all = keep.tile([P, T], U32, name=f"words{a}", align_bytes=64)
-            picked = keep.tile([P, T], U32, name=f"picked_words{a}", align_bytes=64)
-            words.append(w_all)
-            picked_words.append(picked)
-        scalar_share = {(2, 1): 192}
+        picked_a = keep.tile([P, T], U8, name="picked_a", align_bytes=64)
+        picked_bc = keep.tile([P, T], U8, name="picked_bc", align_bytes=64)
+        planes = (bytes_a[:], bytes_bc[:], bytes_bc[4:P, :])
+        picked_planes = (picked_a[:], picked_bc[:], picked_bc[4:P, :])
+        words = [keep.tile([P, T], U32, name=f"words{i}", align_bytes=64) for i in range(3)]
+        picked_words = [keep.tile([P, T], U32, name=f"picked_words{i}", align_bytes=64) for i in range(3)]
 
-        def group_and_quantize(a, h):
-            plane = (bytes01[4:P, :], bytes01[:], bytes2[:])[a]
-            lo = HALF * h
-            grouped = keep.tile([P, HALF, 4], BF16, name=f"grouped{a}_{h}", align_bytes=64)
-            part = [r for r in x_raw[a] if r[0] <= lo < r[1]][0]
-            raw, base = part[2], lo - part[0]
-            cut = scalar_share.get((a, h), 512)
-            for engine, u, v in ((nc.scalar, 0, cut), (nc.vector, cut, HALF)):
+        def group_and_quantize(i, lo, width, scalar):
+            grouped = keep.tile([P, width, 4], BF16, name=f"grouped{i}_{lo}", align_bytes=64)
+            raw = raws[i, lo]
+            for engine, u, v in ((nc.scalar, 0, scalar), (nc.vector, scalar, width)):
                 if u == v:
                     continue
                 dst = grouped[:, u:v, :].rearrange("p (c i) j -> p c j i", i=4)
-                srcv = raw[:, :, base + u : base + v].rearrange("p j (c i) -> p c j i", i=4)
+                src = raw[:, :, u:v].rearrange("p j (c i) -> p c j i", i=4)
                 if engine is nc.scalar:
-                    nc.scalar.copy(dst, srcv)
+                    nc.scalar.copy(dst, src)
                 else:
-                    nc.vector.tensor_copy(dst, srcv)
+                    nc.vector.tensor_copy(dst, src)
             nc.vector.quantize_mx(
-                out=words[a][:, lo : lo + HALF].bitcast(FP8X4),
-                scales=plane[:, lo : lo + HALF],
+                out=words[i][:, lo : lo + width].bitcast(FP8X4),
+                scales=planes[i][:, lo : lo + width],
                 in_=grouped[:].rearrange("p t j -> p (t j)"),
             )
 
         def pick(dst, src, h):
             nc.vector.tensor_copy(dst[:, HALF * h : HALF * (h + 1)], src[:].indirect(offsets[:, 32 * h : 32 * (h + 1)]))
 
-        group_and_quantize(0, 0)
-        group_and_quantize(0, 1)
-        group_and_quantize(1, 0)
-        pick(picked_words[0], words[0], 0)
-        pick(picked_words[0], words[0], 1)
-        group_and_quantize(1, 1)
-        group_and_quantize(2, 0)
-        pick(picked_words[1], words[1], 0)
-        pick(picked_words[1], words[1], 1)
-        pick(picked01, bytes01, 0)
-        pick(picked01, bytes01, 1)
-        group_and_quantize(2, 1)
-        for h in range(2):
-            pick(picked_words[2], words[2], h)
-            pick(picked2, bytes2, h)
+        for i in range(3):
+            for n, chunk in enumerate(CHUNKS[i]):
+                group_and_quantize(i, *chunk)
+                if (i, n) == (2, 0):
+                    pick(picked_a, bytes_a, 0)
+                    pick(picked_a, bytes_a, 1)
+            for h in range(2):
+                pick(picked_words[i], words[i], h)
+                if i == 2:
+                    pick(picked_bc, bytes_bc, h)
 
-        def multiply(acc, m, slot, a):
+        def multiply(acc, m, slot, i):
             e = expert_of(slot)
             n_cols = slice(P * m, P * (m + 1))
             s_cols = slice(slot, slot + CHUNK)
-            if a == 0:
+            if i == 2:
                 lhs = w8[:, e, 4 * P * m : 4 * P * (m + 1)].bitcast(FP8X4)
                 lhs_scale = s8[:, e, n_cols]
             else:
-                lhs = w4[:, e, a - 1, 2 * P * m : 2 * P * (m + 1)].bitcast(FP4X4)
-                lhs_scale = s4[:, 2 * e + a - 1, n_cols]
+                lhs = w4[:, e, i, 2 * P * m : 2 * P * (m + 1)].bitcast(FP4X4)
+                lhs_scale = s4[:, 2 * e + i, n_cols]
             nc.tensor.matmul_mx(
                 out=acc,
                 lhsT=lhs,
                 lhsT_scale=lhs_scale,
-                rhs=picked_words[a][:, s_cols].bitcast(FP8X4),
-                rhs_scale=(picked01[4:P, s_cols], picked01[:, s_cols], picked2[:, s_cols])[a],
-                start=(a == 0),
-                stop=(a == 2),
+                rhs=picked_words[i][:, s_cols].bitcast(FP8X4),
+                rhs_scale=picked_planes[i][:, s_cols],
+                start=(i == 0),
+                stop=(i == 2),
             )
 
         y = [keep.tile([P, T], F32, name=f"y{m}") for m in range(2)]
         result = [keep.tile([P, T], F32, name=f"result{m}") for m in range(2)]
         for h in range(2):
+            slots = range(HALF * h, HALF * (h + 1), CHUNK)
             accs = {}
             for m in range(2):
-                for slot in range(HALF * h, HALF * (h + 1), CHUNK):
+                for slot in slots:
                     acc = psum.tile([P, CHUNK], F32, name="acc")
                     multiply(acc[:], m, slot, 0)
-                    multiply(acc[:], m, slot, 1)
                     accs[m, slot] = acc
+            for i in (1, 2):
+                for m in range(2):
+                    for slot in slots:
+                        multiply(accs[m, slot][:], m, slot, i)
             for m in range(2):
-                for slot in range(HALF * h, HALF * (h + 1), CHUNK):
-                    multiply(accs[m, slot][:], m, slot, 2)
+                for slot in slots:
                     e = expert_of(slot)
-                    nc.scalar.activation(y[m][:, slot : slot + CHUNK], accs[m, slot][:], ACT.Gelu_apprx_tanh, bias=bias[:, m, e : e + 1])
+                    nc.scalar.activation(
+                        y[m][:, slot : slot + CHUNK], accs[m, slot][:], ACT.Gelu_apprx_tanh, bias=bias[:, m, e : e + 1]
+                    )
             for m in range(2):
                 cols = slice(HALF * h, HALF * (h + 1))
-                nc.vector.tensor_tensor(result[m][:].indirect(offsets[:, 32 * h : 32 * (h + 1)]), y[m][:, cols], gates[:, cols], MULT)
+                nc.vector.tensor_tensor(
+                    result[m][:].indirect(offsets[:, 32 * h : 32 * (h + 1)]), y[m][:, cols], gates[:, cols], MULT
+                )
         for m in range(2):
             nc.sync.dma_start(out[P * m : P * (m + 1), :], result[m][:])

@@ -20,7 +20,7 @@ P = 128
 HALF = 512
 CHUNK = 128
 ORDER = (1, 2, 0)
-CHUNKS = (((0, 512, 192), (512, 512, 192),), ((0, 512, 448), (512, 512, 384),), ((0, 512, 448), (512, 256, 192), (768, 256, 160),))
+CHUNKS = (((0, 512, 192), (512, 256, 96), (768, 256, 96),), ((0, 512, 512), (512, 512, 448),), ((0, 512, 448), (512, 256, 192), (768, 256, 128),))
 
 FLOPS = 2 * K * N * T
 BYTES = 4 * K * T + E * (512 * N + 1024 * N // 2 + 48 * N) + 4 * N * E + 4 * T + 2 * P * 64 + 4 * N * T
@@ -36,7 +36,7 @@ def tile_moe_rag_lin_gelu_kernel(
     nc = tc.nc
     with ExitStack() as ctx:
         keep = ctx.enter_context(tc.tile_pool(name="keep", bufs=1))
-        psum = ctx.enter_context(tc.psum_pool(name="psum", bufs=8))
+        psum = ctx.enter_context(tc.psum_pool(name="psum", bufs=6))
 
         offsets = keep.tile([P, T // 16], U16, name="offsets")
 
@@ -150,21 +150,17 @@ def tile_moe_rag_lin_gelu_kernel(
         result = [keep.tile([P, T], F32, name=f"result{m}") for m in range(2)]
         for h in range(2):
             slots = range(HALF * h, HALF * (h + 1), CHUNK)
-            accs = {}
             for m in range(2):
+                accs = {}
                 for slot in slots:
-                    acc = psum.tile([P, CHUNK], F32, name="acc")
-                    multiply(acc[:], m, slot, 0)
-                    accs[m, slot] = acc
-            for i in (1, 2):
-                for m in range(2):
+                    accs[slot] = psum.tile([P, CHUNK], F32, name="acc")
+                for i in range(3):
                     for slot in slots:
-                        multiply(accs[m, slot][:], m, slot, i)
-            for m in range(2):
+                        multiply(accs[slot][:], m, slot, i)
                 for slot in slots:
                     e = expert_of(slot)
                     nc.scalar.activation(
-                        y[m][:, slot : slot + CHUNK], accs[m, slot][:], ACT.Gelu_apprx_tanh, bias=bias[:, m, e : e + 1]
+                        y[m][:, slot : slot + CHUNK], accs[slot][:], ACT.Gelu_apprx_tanh, bias=bias[:, m, e : e + 1]
                     )
             for m in range(2):
                 cols = slice(HALF * h, HALF * (h + 1))

from contextlib import ExitStack

import concourse.mybir as mybir

F32 = mybir.dt.float32
BF16 = mybir.dt.bfloat16
I32 = mybir.dt.int32
U32 = mybir.dt.uint32
U16 = mybir.dt.uint16
U8 = mybir.dt.uint8
FP8X4 = mybir.dt.float8_e4m3fn_x4
FP4X4 = mybir.dt.float4_e2m1fn_x4
ACT = mybir.ActivationFunctionType
MULT = mybir.AluOpType.mult

K, T, E, N = 1536, 1024, 4, 256
COUNTS = (384, 128, 256, 256)
STARTS = (0, 384, 512, 768)
P = 128
HALF = 512
CHUNK = 128
ORDER = (1, 2, 0)
CHUNKS = (((0, 512, 192), (512, 256, 96), (768, 256, 96),), ((0, 512, 512), (512, 512, 448),), ((0, 512, 448), (512, 256, 192), (768, 256, 128),))

FLOPS = 2 * K * N * T
BYTES = 4 * K * T + E * (512 * N + 1024 * N // 2 + 48 * N) + 4 * N * E + 4 * T + 2 * P * 64 + 4 * N * T


def expert_of(slot):
    return max(e for e in range(E) if STARTS[e] <= slot)


def tile_moe_rag_lin_gelu_kernel(
    tc, xT, w8_words, w8_scales, w4_words, w4_scales, b, gate, offs, out
):
    nc = tc.nc
    with ExitStack() as ctx:
        keep = ctx.enter_context(tc.tile_pool(name="keep", bufs=1))
        psum = ctx.enter_context(tc.psum_pool(name="psum", bufs=6))

        offsets = keep.tile([P, T // 16], U16, name="offsets")

        warm = keep.tile([P, 1], F32, name="warm")
        warm_out = keep.tile([P, 1], F32, name="warm_out")
        bytes_a = keep.tile([P, T], U8, name="bytes_a", align_bytes=64)
        bytes_bc = keep.tile([P, T], U8, name="bytes_bc", align_bytes=64)
        s8 = keep.tile([P, E, N], U8, name="s8", align_bytes=64)
        s4 = keep.tile([P, 2 * E, N], U8, name="s4", align_bytes=64)
        nc.gpsimd.memset(warm[:], 0.0)
        nc.gpsimd.memset(bytes_a[:].bitcast(I32), 0)
        nc.gpsimd.memset(bytes_bc[:].bitcast(I32), 0)
        nc.gpsimd.memset(s4[:].rearrange("p e n -> p (e n)").bitcast(I32), 0)
        nc.gpsimd.memset(s8[:].rearrange("p e n -> p (e n)").bitcast(I32), 0)
        nc.scalar.activation(warm_out[:], warm[:], ACT.Gelu_apprx_tanh)

        raws = {}
        for i, a in enumerate(ORDER):
            rows = xT[512 * a : 512 * (a + 1), :].rearrange("(p j) t -> p j t", j=4)
            for lo, width, scalar in CHUNKS[i]:
                raw = keep.tile([P, 4, width], F32, name=f"raw{i}_{lo}")
                nc.sync.dma_start(raw[:], rows[:, :, lo : lo + width])
                raws[i, lo] = raw
            if i == 0:
                nc.sync.dma_start(offsets[:], offs)
        w4s = w4_scales.rearrange("e a q n -> (e a) q n")
        for q in range(4):
            src = w4s[:, 4 * q : 4 * q + 4, :].bitcast(I32)
            nc.sync.dma_start(s4[32 * q : 32 * q + 4, :, :].bitcast(I32), src.rearrange("g r n -> r g n"))
        for q in range(4):
            src = w8_scales[:, 0, 4 * q : 4 * q + 4, :].bitcast(I32)
            nc.sync.dma_start(s8[32 * q : 32 * q + 4, :, :].bitcast(I32), src.rearrange("e r n -> r e n"))
        w8 = keep.tile([P, E, 4 * N], U8, name="w8", align_bytes=64)
        w4 = keep.tile([P, E, 2, 2 * N], U8, name="w4", align_bytes=64)
        gates = keep.tile([P, T], F32, name="gates")
        bias = keep.tile([P, 2, E], F32, name="bias")
        for h in range(2):
            es = slice(2 * h, 2 * h + 2)
            nc.sync.dma_start(
                w4[:, es, :, :].rearrange("p e a x -> p (e a) x").bitcast(I32),
                w4_words.rearrange("e a p x -> (e a) p x")[4 * h : 4 * h + 4].bitcast(I32).rearrange("g p x -> p g x"),
            )
            nc.sync.dma_start(
                w8[:, es, :].bitcast(I32),
                w8_words[es, 0].rearrange("e p n r -> e p (n r)").bitcast(I32).rearrange("e p x -> p e x"),
            )
            if h == 0:
                nc.sync.dma_start(bias[:], b.rearrange("(m p) e -> p m e", p=P))
            nc.sync.dma_start(gates[:, HALF * h : HALF * (h + 1)], gate[0:P, HALF * h : HALF * (h + 1)])

        picked_a = keep.tile([P, T], U8, name="picked_a", align_bytes=64)
        picked_bc = keep.tile([P, T], U8, name="picked_bc", align_bytes=64)
        planes = (bytes_a[:], bytes_bc[:], bytes_bc[4:P, :])
        picked_planes = (picked_a[:], picked_bc[:], picked_bc[4:P, :])
        words = [keep.tile([P, T], U32, name=f"words{i}", align_bytes=64) for i in range(3)]
        picked_words = [keep.tile([P, T], U32, name=f"picked_words{i}", align_bytes=64) for i in range(3)]

        def group_and_quantize(i, lo, width, scalar):
            grouped = keep.tile([P, width, 4], BF16, name=f"grouped{i}_{lo}", align_bytes=64)
            raw = raws[i, lo]
            for engine, u, v in ((nc.scalar, 0, scalar), (nc.vector, scalar, width)):
                if u == v:
                    continue
                dst = grouped[:, u:v, :].rearrange("p (c i) j -> p c j i", i=4)
                src = raw[:, :, u:v].rearrange("p j (c i) -> p c j i", i=4)
                if engine is nc.scalar:
                    nc.scalar.copy(dst, src)
                else:
                    nc.vector.tensor_copy(dst, src)
            nc.vector.quantize_mx(
                out=words[i][:, lo : lo + width].bitcast(FP8X4),
                scales=planes[i][:, lo : lo + width],
                in_=grouped[:].rearrange("p t j -> p (t j)"),
            )

        def pick(dst, src, h):
            nc.vector.tensor_copy(dst[:, HALF * h : HALF * (h + 1)], src[:].indirect(offsets[:, 32 * h : 32 * (h + 1)]))

        for i in range(3):
            for n, chunk in enumerate(CHUNKS[i]):
                group_and_quantize(i, *chunk)
                if (i, n) == (2, 0):
                    pick(picked_a, bytes_a, 0)
                    pick(picked_a, bytes_a, 1)
            for h in range(2):
                pick(picked_words[i], words[i], h)
                if i == 2:
                    pick(picked_bc, bytes_bc, h)

        def multiply(acc, m, slot, i):
            e = expert_of(slot)
            n_cols = slice(P * m, P * (m + 1))
            s_cols = slice(slot, slot + CHUNK)
            if i == 2:
                lhs = w8[:, e, 4 * P * m : 4 * P * (m + 1)].bitcast(FP8X4)
                lhs_scale = s8[:, e, n_cols]
            else:
                lhs = w4[:, e, i, 2 * P * m : 2 * P * (m + 1)].bitcast(FP4X4)
                lhs_scale = s4[:, 2 * e + i, n_cols]
            nc.tensor.matmul_mx(
                out=acc,
                lhsT=lhs,
                lhsT_scale=lhs_scale,
                rhs=picked_words[i][:, s_cols].bitcast(FP8X4),
                rhs_scale=picked_planes[i][:, s_cols],
                start=(i == 0),
                stop=(i == 2),
            )

        y = [keep.tile([P, T], F32, name=f"y{m}") for m in range(2)]
        result = [keep.tile([P, T], F32, name=f"result{m}") for m in range(2)]
        for h in range(2):
            slots = range(HALF * h, HALF * (h + 1), CHUNK)
            for m in range(2):
                accs = {}
                for slot in slots:
                    accs[slot] = psum.tile([P, CHUNK], F32, name="acc")
                for i in range(3):
                    for slot in slots:
                        multiply(accs[slot][:], m, slot, i)
                for slot in slots:
                    e = expert_of(slot)
                    nc.scalar.activation(
                        y[m][:, slot : slot + CHUNK], accs[slot][:], ACT.Gelu_apprx_tanh, bias=bias[:, m, e : e + 1]
                    )
            for m in range(2):
                cols = slice(HALF * h, HALF * (h + 1))
                nc.vector.tensor_tensor(
                    result[m][:].indirect(offsets[:, 32 * h : 32 * (h + 1)]), y[m][:, cols], gates[:, cols], MULT
                )
        for m in range(2):
            nc.sync.dma_start(out[P * m : P * (m + 1), :], result[m][:])
